import numpy as np
import ml_dtypes


def mxq(x, axis, fmt="e4m3"):
    dtype, down = {"e4m3": (ml_dtypes.float8_e4m3fn, 7), "e5m2": (ml_dtypes.float8_e5m2, 14)}[fmt]
    v = np.moveaxis(np.asarray(x, np.float32).astype(ml_dtypes.bfloat16).astype(np.float64), axis, -1)
    blocks = v.reshape(v.shape[:-1] + (-1, 32))
    amax = np.abs(blocks).max(-1, keepdims=True)
    byte = np.maximum(np.where(amax > 0, np.frexp(amax)[1] - 1 + 127, 0) - down, 1)
    scale = np.exp2(byte - 127.0)
    codes = (blocks / scale).astype(np.float32).astype(dtype).astype(np.float64)
    return np.moveaxis((codes * scale).reshape(v.shape), -1, axis)


WIDE = False


def mx_kscale(k):
    if not WIDE:
        return np.ones(k)
    levels = np.array([10, -10, 5, -5, 0])
    if k % 512:
        return np.exp2(np.random.permutation(np.resize(levels, k // 32))).repeat(32)
    a = np.empty((k // 512, 16))
    for p in range(k // 512):
        a[p, :8] = np.random.permutation(np.resize(levels, 8))
        for g in range(8):
            far = levels[np.abs(levels - a[p, g]) >= 10]
            a[p, g + 8] = far[np.random.randint(len(far))]
    return np.exp2(a.ravel()).repeat(32)


def f64(x):
    return np.asarray(x).astype(np.float64)


def striped(idx):
    return np.tile(np.asarray(idx).reshape(-1, 16).T, (8, 1)).astype(np.uint16)


def unstriped(offs):
    return offs[:16].T.reshape(-1).astype(np.int64)


E2M1 = np.array([0.0, 0.5, 1.0, 1.5, 2.0, 3.0, 4.0, 6.0, -0.0, -0.5, -1.0, -1.5, -2.0, -3.0, -4.0, -6.0])


def pack_weight(w, fmt):
    k, n = w.shape
    w = f64(np.asarray(w, np.float32).astype(ml_dtypes.bfloat16)).reshape(k // 32, 32, n)
    amax = np.abs(w).max(1)
    if fmt == "e4m3":
        byte = np.frexp(amax)[1] - 1 + 127 - 7
    else:
        mant, ex = np.frexp(amax / 6.0)
        byte = np.where(mant > 0.5, ex, ex - 1) + 127
    byte = np.clip(np.where(amax > 0, byte, 1), 1, 254)
    scaled = (w * np.exp2(127.0 - byte)[:, None, :]).reshape(k, n).astype(np.float32)
    by_word = np.ascontiguousarray(scaled.reshape(k // 512, 128, 4, n).transpose(0, 1, 3, 2))
    if fmt == "e4m3":
        words = by_word.astype(ml_dtypes.float8_e4m3fn).view(np.uint8)
    else:
        c = by_word.astype(ml_dtypes.float4_e2m1fn).view(np.uint8) & 0xF
        words = (c[..., 0::2] | (c[..., 1::2] << 4)).reshape(k // 512, 128, 2 * n)
    return np.ascontiguousarray(words), np.ascontiguousarray(byte.astype(np.uint8).reshape(k // 512, 16, n))


def unpack_weight(words, scales, fmt):
    g, _, n = scales.shape
    words = np.ascontiguousarray(words).reshape(g, 128, n, -1)
    if fmt == "e4m3":
        vals = words.view(ml_dtypes.float8_e4m3fn).astype(np.float64)
    else:
        nib = np.empty((g, 128, n, 4), np.uint8)
        nib[..., 0::2] = words & 0xF
        nib[..., 1::2] = words >> 4
        vals = E2M1[nib]
    vals = vals * np.repeat(np.exp2(scales.astype(np.float64) - 127.0), 8, axis=1)[..., None]
    return vals.transpose(0, 1, 3, 2).reshape(g * 512, n)


K, T, J, B, R, N = 512, 2048, 512, 128, 512, 512


def setup_inputs():
    n = np.random.standard_normal
    idx = np.random.permutation(T)[:J]
    fk = mx_kscale(K)
    fr = mx_kscale(R)
    xtp = pack_weight(n((K, T)) / fk[:, None], "e4m3")
    wap = pack_weight(n((K, R)) * 1 / np.sqrt(K) * fk[:, None] * fr, "e2m1")
    wbp = pack_weight(n((R, N)) * 1 / np.sqrt(R) / fr[:, None], "e4m3")
    return {
        "xt_words": xtp[0],
        "xt_scales": xtp[1],
        "wa_words": wap[0],
        "wa_scales": wap[1],
        "wb_words": wbp[0],
        "wb_scales": wbp[1],
        "rw": (np.random.uniform(0.5, 2.0, (1, J))).astype(np.float32),
        "offs": striped(idx),
    }


def reference(xt_words, xt_scales, wa_words, wa_scales, wb_words, wb_scales, rw, offs):
    idx = unstriped(offs)
    xtu = unpack_weight(xt_words, xt_scales, "e4m3")
    wau = unpack_weight(wa_words, wa_scales, "e2m1")
    wbu = unpack_weight(wb_words, wb_scales, "e4m3")
    xtidxg = xtu[:, idx]
    a = wau.T @ xtidxg
    m1 = a.reshape(R, B, J // B).mean(axis=2)
    mr1 = np.repeat(m1, J // B, axis=1)
    hid = a - mr1
    hidq = mxq(hid, 0, "e4m3")
    p = wbu.T @ hidq
    y = p * f64(rw)
    return y

@@ -1,0 +1,196 @@
+from contextlib import ExitStack
+
+import concourse.mybir as mybir
+from concourse.masks import make_identity
+
+K, T, J, R, N = 512, 2048, 512, 512, 512
+FLOPS = 2 * K * R * J + 2 * R * N * J
+
+F32 = mybir.dt.float32
+BF16 = mybir.dt.bfloat16
+I32 = mybir.dt.int32
+U32 = mybir.dt.uint32
+U16 = mybir.dt.uint16
+U8 = mybir.dt.uint8
+FP8X4 = mybir.dt.float8_e4m3fn_x4
+FP4X4 = mybir.dt.float4_e2m1fn_x4
+ALU = mybir.AluOpType
+ACT = mybir.ActivationFunctionType
+
+P = 128
+PACK = 4
+GROUP = 4
+CHUNK = 128
+HALF = 256
+CHUNKS = J // CHUNK
+
+
+def load_scale_rows(queue, plane, scales, quadrant):
+    queue.dma_start(
+        out=plane[32 * quadrant : 32 * quadrant + 4, :].bitcast(I32),
+        in_=scales[0, 4 * quadrant : 4 * quadrant + 4, :].bitcast(I32),
+    )
+
+
+def tile_list_hidden_relative_to_group_kernel(
+    tc, xt_words, xt_scales, wa_words, wa_scales, wb_words, wb_scales, rw, offs, out
+):
+    nc = tc.nc
+    with ExitStack() as ctx:
+        keep = ctx.enter_context(tc.tile_pool(name="keep", bufs=1))
+        psum = ctx.enter_context(tc.psum_pool(name="psum", bufs=1))
+
+        offsets = keep.tile([P, J // 16], U16, name="offsets")
+        nc.sync.dma_start(offsets[:], offs)
+        wa_raw = keep.tile([P, 2 * R], U8, name="wa_raw", tag="weights_in", align_bytes=64)
+        nc.sync.dma_start(out=wa_raw[:].bitcast(I32), in_=wa_words[0].bitcast(I32))
+        was_raw = keep.tile([P, R], U8, name="was_raw", tag="late", align_bytes=64)
+        nc.scalar.dma_start(
+            out=was_raw[96:128, :].bitcast(I32),
+            in_=wa_scales[0, 12:16, :].bitcast(I32).unsqueeze(0).to_broadcast([8, 4, R // 4]),
+        )
+
+        xs_window = keep.tile([P, T], U8, name="xs_window", align_bytes=64)
+        wb_plane = keep.tile([P, N], U8, name="wb_plane", align_bytes=64)
+        nc.gpsimd.memset(xs_window[:, T // 2 :].bitcast(I32), 0)
+        for plane in (xs_window[:, : T // 2], was_raw[0:96, :], wb_plane[:]):
+            nc.vector.memset(plane.bitcast(I32), 0)
+        for q in range(4):
+            load_scale_rows(nc.sync if q < 2 else nc.scalar, xs_window, xt_scales, q)
+        x_window = keep.tile([P, T], U32, name="x_window", align_bytes=64)
+        nc.sync.dma_start(
+            out=x_window[:].bitcast(I32), in_=xt_words[0].rearrange("p c t -> p (c t)").bitcast(I32)
+        )
+        for q in range(3):
+            load_scale_rows(nc.sync, was_raw, wa_scales, q)
+        for q in range(4):
+            load_scale_rows(nc.sync, wb_plane, wb_scales, q)
+
+        rw_cols = keep.tile([P, GROUP], F32, name="rw_cols")
+        nc.gpsimd.dma_start(out=rw_cols[:], in_=rw.rearrange("o (b i) -> (o b) i", i=GROUP))
+        ident = keep.tile([P, P], F32, name="ident")
+        make_identity(nc, ident[:])
+        rw_bank = psum.tile([P, GROUP, P], F32, name="rw_bank", tag="p3")
+        for i in range(GROUP):
+            nc.tensor.transpose(rw_bank[:, i, :], rw_cols[:, i : i + 1].to_broadcast([P, P]), ident[:])
+        rw_rows = keep.tile([P, J], F32, name="rw_rows", align_bytes=64)
+        nc.scalar.copy(
+            out=rw_rows[:].rearrange("p (b i) -> p b i", i=GROUP), in_=rw_bank[:].rearrange("p i b -> p b i")
+        )
+
+        wa_codes = keep.tile([P, 2 * R], U8, name="wa_codes", align_bytes=64)
+        nc.vector.tensor_copy(
+            out=wa_codes[:].bitcast(U16).rearrange("p (t m) -> p t m", t=PACK),
+            in_=wa_raw[:].bitcast(U16).rearrange("p (m t) -> p t m", t=PACK),
+        )
+        wb_codes = keep.tile([P, N], U32, name="wb_codes", tag="weights_in", align_bytes=64)
+        nc.sync.dma_start(
+            out=wb_codes[:].bitcast(I32), in_=wb_words[0].rearrange("p c t -> p (c t)").bitcast(I32)
+        )
+
+        x_codes, x_plane = [], []
+        for h in range(2):
+            x_plane.append(keep.tile([P, HALF], U8, name="x_plane%d" % h, align_bytes=64))
+        lists = [offsets[:, 16 * h : 16 * h + 16] for h in range(2)]
+        nc.vector.tensor_copy(x_plane[0][:], xs_window[:].indirect(lists[0]))
+        nc.vector.tensor_copy(x_plane[1][:], xs_window[:].indirect(lists[1]))
+        wa_plane = keep.tile([P, R], U8, name="wa_plane", align_bytes=64)
+        nc.vector.tensor_copy(
+            out=wa_plane[:].rearrange("p (t m) -> p t m", t=PACK),
+            in_=was_raw[:].rearrange("p (m t) -> p t m", t=PACK),
+        )
+        x_codes.append(keep.tile([P, HALF], U32, name="x_codes0", align_bytes=64))
+        x_codes.append(keep.tile([P, HALF], U32, name="x_codes1", tag="late", align_bytes=64))
+        nc.vector.tensor_copy(x_codes[0][:], x_window[:].indirect(lists[0]))
+        nc.vector.tensor_copy(x_codes[1][:], x_window[:].indirect(lists[1]))
+
+        out_view = out.rearrange("(u p) j -> p u j", p=P)
+        a_bank, mean, hid_codes, hid_plane, hid = {}, {}, {}, {}, {}
+
+        def first_product(c):
+            h, cols = c // 2, slice((c % 2) * CHUNK, (c % 2 + 1) * CHUNK)
+            a_bank[c] = psum.tile([P, PACK, CHUNK], F32, name="a%d" % c)
+            for t in range(PACK):
+                nc.tensor.matmul_mx(
+                    out=a_bank[c][:, t, :],
+                    lhsT=wa_codes[:, 2 * P * t : 2 * P * (t + 1)].bitcast(FP4X4),
+                    lhsT_scale=wa_plane[:, P * t : P * (t + 1)],
+                    rhs=x_codes[h][:, cols].bitcast(FP8X4),
+                    rhs_scale=x_plane[h][:, cols],
+                    start=True,
+                    stop=True,
+                )
+
+        def group_mean(c):
+            total = keep.tile([P, CHUNK // GROUP, PACK], F32, name="total%d" % c)
+            nc.vector.tensor_reduce(
+                out=total[:],
+                in_=a_bank[c][:].rearrange("p t (b i) -> p b t i", i=GROUP),
+                axis=mybir.AxisListType.X,
+                op=ALU.add,
+            )
+            mean[c] = keep.tile([P, CHUNK // GROUP, PACK], F32, name="mean%d" % c)
+            nc.scalar.activation(out=mean[c][:], in_=total[:], func=ACT.Copy, scale=1.0 / GROUP)
+
+        def subtract(c):
+            hid[c] = keep.tile([P, CHUNK * PACK], BF16, name="hid%d" % c, align_bytes=64)
+            nc.vector.tensor_tensor(
+                out=hid[c][:].rearrange("p (b i t) -> p b i t", i=GROUP, t=PACK),
+                in0=a_bank[c][:].rearrange("p t (b i) -> p b i t", i=GROUP),
+                in1=mean[c][:].unsqueeze(2).to_broadcast([P, CHUNK // GROUP, GROUP, PACK]),
+                op=ALU.subtract,
+            )
+
+        def quantise(c):
+            hid_codes[c] = keep.tile([P, CHUNK], U32, name="hid_codes%d" % c, align_bytes=64)
+            hid_plane[c] = keep.tile([P, CHUNK], U8, name="hid_plane%d" % c, align_bytes=64)
+            nc.vector.quantize_mx(out=hid_codes[c][:].bitcast(FP8X4), scales=hid_plane[c][:], in_=hid[c][:])
+
+        p_bank = {}
+
+        def second_product(c):
+            p_bank[c] = psum.tile([P, N // P, CHUNK], F32, name="p%d" % c, tag="p%d" % c)
+            for u in range(N // P):
+                nc.tensor.matmul_mx(
+                    out=p_bank[c][:, u, :],
+                    lhsT=wb_codes[:, P * u : P * (u + 1)].bitcast(FP8X4),
+                    lhsT_scale=wb_plane[:, P * u : P * (u + 1)],
+                    rhs=hid_codes[c][:].bitcast(FP8X4),
+                    rhs_scale=hid_plane[c][:],
+                    start=True,
+                    stop=True,
+                )
+
+        def weigh_and_store(c):
+            cols = slice(c * CHUNK, (c + 1) * CHUNK)
+            result = keep.tile([P, N // P, CHUNK], F32, name="result%d" % c)
+            nc.vector.tensor_tensor(
+                out=result[:],
+                in0=p_bank[c][:],
+                in1=rw_rows[:, cols].unsqueeze(1).to_broadcast([P, N // P, CHUNK]),
+                op=ALU.mult,
+            )
+            nc.sync.dma_start(out=out_view[:, :, cols], in_=result[:])
+
+        for c in range(CHUNKS):
+            first_product(c)
+        group_mean(0)
+        group_mean(1)
+        subtract(0)
+        group_mean(2)
+        quantise(0)
+        second_product(0)
+        subtract(1)
+        group_mean(3)
+        quantise(1)
+        second_product(1)
+        subtract(2)
+        weigh_and_store(0)
+        quantise(2)
+        second_product(2)
+        subtract(3)
+        weigh_and_store(1)
+        quantise(3)
+        second_product(3)
+        weigh_and_store(2)
+        weigh_and_store(3)

@@ -1,7 +1,6 @@
 from contextlib import ExitStack
 
 import concourse.mybir as mybir
-from concourse.masks import make_identity
 
 K, T, J, R, N = 512, 2048, 512, 512, 512
 FLOPS = 2 * K * R * J + 2 * R * N * J
@@ -50,7 +49,7 @@ def tile_list_hidden_relative_to_group_kernel(
             in_=wa_scales[0, 12:16, :].bitcast(I32).unsqueeze(0).to_broadcast([8, 4, R // 4]),
         )
 
-        xs_window = keep.tile([P, T], U8, name="xs_window", align_bytes=64)
+        xs_window = keep.tile([P, T], U8, name="xs_window", tag="rows", align_bytes=64)
         wb_plane = keep.tile([P, N], U8, name="wb_plane", align_bytes=64)
         nc.gpsimd.memset(xs_window[:, T // 2 :].bitcast(I32), 0)
         for plane in (xs_window[:, : T // 2], was_raw[0:96, :], wb_plane[:]):
@@ -66,17 +65,6 @@ def tile_list_hidden_relative_to_group_kernel(
         for q in range(4):
             load_scale_rows(nc.sync, wb_plane, wb_scales, q)
 
-        rw_cols = keep.tile([P, GROUP], F32, name="rw_cols")
-        nc.gpsimd.dma_start(out=rw_cols[:], in_=rw.rearrange("o (b i) -> (o b) i", i=GROUP))
-        ident = keep.tile([P, P], F32, name="ident")
-        make_identity(nc, ident[:])
-        rw_bank = psum.tile([P, GROUP, P], F32, name="rw_bank", tag="p3")
-        for i in range(GROUP):
-            nc.tensor.transpose(rw_bank[:, i, :], rw_cols[:, i : i + 1].to_broadcast([P, P]), ident[:])
-        rw_rows = keep.tile([P, J], F32, name="rw_rows", align_bytes=64)
-        nc.scalar.copy(
-            out=rw_rows[:].rearrange("p (b i) -> p b i", i=GROUP), in_=rw_bank[:].rearrange("p i b -> p b i")
-        )
 
         wa_codes = keep.tile([P, 2 * R], U8, name="wa_codes", align_bytes=64)
         nc.vector.tensor_copy(
@@ -94,6 +82,8 @@ def tile_list_hidden_relative_to_group_kernel(
         lists = [offsets[:, 16 * h : 16 * h + 16] for h in range(2)]
         nc.vector.tensor_copy(x_plane[0][:], xs_window[:].indirect(lists[0]))
         nc.vector.tensor_copy(x_plane[1][:], xs_window[:].indirect(lists[1]))
+        rw_rows = keep.tile([P, J], F32, name="rw_rows", tag="rows", align_bytes=64)
+        nc.sync.dma_start(out=rw_rows[:], in_=rw[0].partition_broadcast(P))
         wa_plane = keep.tile([P, R], U8, name="wa_plane", align_bytes=64)
         nc.vector.tensor_copy(
             out=wa_plane[:].rearrange("p (t m) -> p t m", t=PACK),
@@ -109,7 +99,7 @@ def tile_list_hidden_relative_to_group_kernel(
 
         def first_product(c):
             h, cols = c // 2, slice((c % 2) * CHUNK, (c % 2 + 1) * CHUNK)
-            a_bank[c] = psum.tile([P, PACK, CHUNK], F32, name="a%d" % c)
+            a_bank[c] = psum.tile([P, PACK, CHUNK], F32, name="a%d" % c, tag="a%d" % c)
             for t in range(PACK):
                 nc.tensor.matmul_mx(
                     out=a_bank[c][:, t, :],
@@ -131,6 +121,21 @@ def tile_list_hidden_relative_to_group_kernel(
             )
             mean[c] = keep.tile([P, CHUNK // GROUP, PACK], F32, name="mean%d" % c)
             nc.scalar.activation(out=mean[c][:], in_=total[:], func=ACT.Copy, scale=1.0 / GROUP)
+
+        def group_mean_aside(c):
+            quarter = keep.tile([P, GROUP, CHUNK], F32, name="quarter%d" % c)
+            nc.scalar.activation(
+                out=quarter[:].rearrange("p i (b t) -> p i b t", t=PACK),
+                in_=a_bank[c][:].rearrange("p t (b i) -> p i b t", i=GROUP),
+                func=ACT.Copy,
+                scale=1.0 / GROUP,
+            )
+            pair = keep.tile([P, 2, CHUNK], F32, name="pair%d" % c)
+            nc.gpsimd.tensor_tensor(out=pair[:], in0=quarter[:, 0:2, :], in1=quarter[:, 2:4, :], op=ALU.add)
+            mean[c] = keep.tile([P, CHUNK // GROUP, PACK], F32, name="mean%d" % c)
+            nc.gpsimd.tensor_tensor(
+                out=mean[c][:].rearrange("p b t -> p (b t)"), in0=pair[:, 0, :], in1=pair[:, 1, :], op=ALU.add
+            )
 
         def subtract(c):
             hid[c] = keep.tile([P, CHUNK * PACK], BF16, name="hid%d" % c, align_bytes=64)
@@ -161,6 +166,34 @@ def tile_list_hidden_relative_to_group_kernel(
                     stop=True,
                 )
 
+        def last_product(c):
+            halves = []
+            for h, tag in enumerate(("p%d" % c, "a0")):
+                halves.append(psum.tile([P, 2, CHUNK], F32, name="last%d" % h, tag=tag))
+                for u in range(2 * h, 2 * h + 2):
+                    nc.tensor.matmul_mx(
+                        out=halves[h][:, u - 2 * h, :],
+                        lhsT=wb_codes[:, P * u : P * (u + 1)].bitcast(FP8X4),
+                        lhsT_scale=wb_plane[:, P * u : P * (u + 1)],
+                        rhs=hid_codes[c][:].bitcast(FP8X4),
+                        rhs_scale=hid_plane[c][:],
+                        start=True,
+                        stop=True,
+                    )
+            p_bank[c] = halves
+
+        def last_weigh_and_store(c):
+            cols = slice(c * CHUNK, (c + 1) * CHUNK)
+            for h, queue in enumerate((nc.sync, nc.scalar)):
+                result = keep.tile([P, 2, CHUNK], F32, name="last_result%d" % h)
+                nc.vector.tensor_tensor(
+                    out=result[:],
+                    in0=p_bank[c][h][:],
+                    in1=rw_rows[:, cols].unsqueeze(1).to_broadcast([P, 2, CHUNK]),
+                    op=ALU.mult,
+                )
+                queue.dma_start(out=out_view[:, 2 * h : 2 * h + 2, cols], in_=result[:])
+
         def weigh_and_store(c):
             cols = slice(c * CHUNK, (c + 1) * CHUNK)
             result = keep.tile([P, N // P, CHUNK], F32, name="result%d" % c)
@@ -176,12 +209,12 @@ def tile_list_hidden_relative_to_group_kernel(
             first_product(c)
         group_mean(0)
         group_mean(1)
+        group_mean_aside(3)
         subtract(0)
         group_mean(2)
         quantise(0)
         second_product(0)
         subtract(1)
-        group_mean(3)
         quantise(1)
         second_product(1)
         subtract(2)
@@ -191,6 +224,6 @@ def tile_list_hidden_relative_to_group_kernel(
         subtract(3)
         weigh_and_store(1)
         quantise(3)
-        second_product(3)
+        last_product(3)
         weigh_and_store(2)
-        weigh_and_store(3)
+        last_weigh_and_store(3)

@@ -31,6 +31,14 @@ def load_scale_rows(queue, plane, scales, quadrant):
     )
 
 
+def fill_scale_quadrant(queue, plane, scales, quadrant):
+    width = scales.shape[2] // 4
+    queue.dma_start(
+        out=plane[32 * quadrant : 32 * quadrant + 32, :].bitcast(I32),
+        in_=scales[0, 4 * quadrant : 4 * quadrant + 4, :].bitcast(I32).unsqueeze(0).to_broadcast([8, 4, width]),
+    )
+
+
 def tile_list_hidden_relative_to_group_kernel(
     tc, xt_words, xt_scales, wa_words, wa_scales, wb_words, wb_scales, rw, offs, out
 ):
@@ -40,59 +48,54 @@ def tile_list_hidden_relative_to_group_kernel(
         psum = ctx.enter_context(tc.psum_pool(name="psum", bufs=1))
 
         offsets = keep.tile([P, J // 16], U16, name="offsets")
-        nc.sync.dma_start(offsets[:], offs)
-        wa_raw = keep.tile([P, 2 * R], U8, name="wa_raw", tag="weights_in", align_bytes=64)
-        nc.sync.dma_start(out=wa_raw[:].bitcast(I32), in_=wa_words[0].bitcast(I32))
         was_raw = keep.tile([P, R], U8, name="was_raw", tag="late", align_bytes=64)
-        nc.scalar.dma_start(
-            out=was_raw[96:128, :].bitcast(I32),
-            in_=wa_scales[0, 12:16, :].bitcast(I32).unsqueeze(0).to_broadcast([8, 4, R // 4]),
-        )
-
-        xs_window = keep.tile([P, T], U8, name="xs_window", tag="rows", align_bytes=64)
-        wb_plane = keep.tile([P, N], U8, name="wb_plane", align_bytes=64)
-        nc.gpsimd.memset(xs_window[:, T // 2 :].bitcast(I32), 0)
-        for plane in (xs_window[:, : T // 2], was_raw[0:96, :], wb_plane[:]):
-            nc.vector.memset(plane.bitcast(I32), 0)
-        for q in range(4):
-            load_scale_rows(nc.sync if q < 2 else nc.scalar, xs_window, xt_scales, q)
         x_window = keep.tile([P, T], U32, name="x_window", align_bytes=64)
-        nc.sync.dma_start(
-            out=x_window[:].bitcast(I32), in_=xt_words[0].rearrange("p c t -> p (c t)").bitcast(I32)
-        )
-        for q in range(3):
-            load_scale_rows(nc.sync, was_raw, wa_scales, q)
-        for q in range(4):
-            load_scale_rows(nc.sync, wb_plane, wb_scales, q)
-
-
         wa_codes = keep.tile([P, 2 * R], U8, name="wa_codes", align_bytes=64)
-        nc.vector.tensor_copy(
-            out=wa_codes[:].bitcast(U16).rearrange("p (t m) -> p t m", t=PACK),
-            in_=wa_raw[:].bitcast(U16).rearrange("p (m t) -> p t m", t=PACK),
-        )
-        wb_codes = keep.tile([P, N], U32, name="wb_codes", tag="weights_in", align_bytes=64)
+        x_plane = [keep.tile([P, HALF], U8, name="x_plane%d" % h, align_bytes=64) for h in range(2)]
+        lists = [offsets[:, 16 * h : 16 * h + 16] for h in range(2)]
+        with tc.tile_pool(name="early", bufs=1) as early:
+            wa_raw = early.tile([P, 2 * R], U8, name="wa_raw", align_bytes=64)
+            xs_window = early.tile([P, T], U8, name="xs_window", align_bytes=64)
+            nc.sync.dma_start(offsets[:], offs)
+            nc.sync.dma_start(out=wa_raw[:].bitcast(I32), in_=wa_words[0].bitcast(I32))
+            fill_scale_quadrant(nc.scalar, was_raw, wa_scales, 3)
+            nc.gpsimd.memset(xs_window[:, T // 2 :].bitcast(I32), 0)
+            for plane in (xs_window[:, : T // 2], was_raw[0:96, :]):
+                nc.vector.memset(plane.bitcast(I32), 0)
+            for q in range(4):
+                load_scale_rows(nc.sync if q < 2 else nc.scalar, xs_window, xt_scales, q)
+            nc.scalar.dma_start(
+                out=x_window[:].bitcast(I32), in_=xt_words[0].rearrange("p c t -> p (c t)").bitcast(I32)
+            )
+            for q in range(3):
+                load_scale_rows(nc.sync, was_raw, wa_scales, q)
+            nc.vector.tensor_copy(
+                out=wa_codes[:].bitcast(U16).rearrange("p (t m) -> p t m", t=PACK),
+                in_=wa_raw[:].bitcast(U16).rearrange("p (m t) -> p t m", t=PACK),
+            )
+            for h in range(2):
+                nc.vector.tensor_copy(x_plane[h][:], xs_window[:].indirect(lists[h]))
+
+        later = ctx.enter_context(tc.tile_pool(name="later", bufs=1))
+        wb_codes = later.tile([P, N], U32, name="wb_codes", align_bytes=64)
+        wb_plane = later.tile([P, N], U8, name="wb_plane", align_bytes=64)
+        rw_rows = later.tile([P, J], F32, name="rw_rows", align_bytes=64)
         nc.sync.dma_start(
             out=wb_codes[:].bitcast(I32), in_=wb_words[0].rearrange("p c t -> p (c t)").bitcast(I32)
         )
-
-        x_codes, x_plane = [], []
-        for h in range(2):
-            x_plane.append(keep.tile([P, HALF], U8, name="x_plane%d" % h, align_bytes=64))
-        lists = [offsets[:, 16 * h : 16 * h + 16] for h in range(2)]
-        nc.vector.tensor_copy(x_plane[0][:], xs_window[:].indirect(lists[0]))
-        nc.vector.tensor_copy(x_plane[1][:], xs_window[:].indirect(lists[1]))
-        rw_rows = keep.tile([P, J], F32, name="rw_rows", tag="rows", align_bytes=64)
+        for q in range(4):
+            fill_scale_quadrant(nc.sync, wb_plane, wb_scales, q)
         nc.sync.dma_start(out=rw_rows[:], in_=rw[0].partition_broadcast(P))
+
         wa_plane = keep.tile([P, R], U8, name="wa_plane", align_bytes=64)
         nc.vector.tensor_copy(
             out=wa_plane[:].rearrange("p (t m) -> p t m", t=PACK),
             in_=was_raw[:].rearrange("p (m t) -> p t m", t=PACK),
         )
-        x_codes.append(keep.tile([P, HALF], U32, name="x_codes0", align_bytes=64))
-        x_codes.append(keep.tile([P, HALF], U32, name="x_codes1", tag="late", align_bytes=64))
-        nc.vector.tensor_copy(x_codes[0][:], x_window[:].indirect(lists[0]))
-        nc.vector.tensor_copy(x_codes[1][:], x_window[:].indirect(lists[1]))
+        picked = keep.tile([P, J], U32, name="picked", tag="late", align_bytes=64)
+        x_codes = [picked[:, HALF * h : HALF * (h + 1)] for h in range(2)]
+        for h in range(2):
+            nc.vector.tensor_copy(x_codes[h], x_window[:].indirect(lists[h]))
 
         out_view = out.rearrange("(u p) j -> p u j", p=P)
         a_bank, mean, hid_codes, hid_plane, hid = {}, {}, {}, {}, {}

from contextlib import ExitStack

import concourse.mybir as mybir

K, T, J, R, N = 512, 2048, 512, 512, 512
FLOPS = 2 * K * R * J + 2 * R * N * J

F32 = mybir.dt.float32
BF16 = mybir.dt.bfloat16
I32 = mybir.dt.int32
U32 = mybir.dt.uint32
U16 = mybir.dt.uint16
U8 = mybir.dt.uint8
FP8X4 = mybir.dt.float8_e4m3fn_x4
FP4X4 = mybir.dt.float4_e2m1fn_x4
ALU = mybir.AluOpType
ACT = mybir.ActivationFunctionType

P = 128
PACK = 4
GROUP = 4
CHUNK = 128
HALF = 256
CHUNKS = J // CHUNK


def load_scale_rows(queue, plane, scales, quadrant):
    queue.dma_start(
        out=plane[32 * quadrant : 32 * quadrant + 4, :].bitcast(I32),
        in_=scales[0, 4 * quadrant : 4 * quadrant + 4, :].bitcast(I32),
    )


def fill_scale_quadrant(queue, plane, scales, quadrant):
    width = scales.shape[2] // 4
    queue.dma_start(
        out=plane[32 * quadrant : 32 * quadrant + 32, :].bitcast(I32),
        in_=scales[0, 4 * quadrant : 4 * quadrant + 4, :].bitcast(I32).unsqueeze(0).to_broadcast([8, 4, width]),
    )


def tile_list_hidden_relative_to_group_kernel(
    tc, xt_words, xt_scales, wa_words, wa_scales, wb_words, wb_scales, rw, offs, out
):
    nc = tc.nc
    with ExitStack() as ctx:
        keep = ctx.enter_context(tc.tile_pool(name="keep", bufs=1))
        psum = ctx.enter_context(tc.psum_pool(name="psum", bufs=1))

        offsets = keep.tile([P, J // 16], U16, name="offsets")
        was_raw = keep.tile([P, R], U8, name="was_raw", tag="late", align_bytes=64)
        x_window = keep.tile([P, T], U32, name="x_window", align_bytes=64)
        wa_codes = keep.tile([P, 2 * R], U8, name="wa_codes", align_bytes=64)
        x_plane = [keep.tile([P, HALF], U8, name="x_plane%d" % h, align_bytes=64) for h in range(2)]
        lists = [offsets[:, 16 * h : 16 * h + 16] for h in range(2)]
        with tc.tile_pool(name="early", bufs=1) as early:
            wa_raw = early.tile([P, 2 * R], U8, name="wa_raw", align_bytes=64)
            xs_window = early.tile([P, T], U8, name="xs_window", align_bytes=64)
            nc.sync.dma_start(offsets[:], offs)
            nc.sync.dma_start(out=wa_raw[:].bitcast(I32), in_=wa_words[0].bitcast(I32))
            fill_scale_quadrant(nc.scalar, was_raw, wa_scales, 3)
            nc.gpsimd.memset(xs_window[:, T // 2 :].bitcast(I32), 0)
            for plane in (xs_window[:, : T // 2], was_raw[0:96, :]):
                nc.vector.memset(plane.bitcast(I32), 0)
            for q in range(4):
                load_scale_rows(nc.sync if q < 2 else nc.scalar, xs_window, xt_scales, q)
            nc.scalar.dma_start(
                out=x_window[:].bitcast(I32), in_=xt_words[0].rearrange("p c t -> p (c t)").bitcast(I32)
            )
            for q in range(3):
                load_scale_rows(nc.sync, was_raw, wa_scales, q)
            nc.vector.tensor_copy(
                out=wa_codes[:].bitcast(U16).rearrange("p (t m) -> p t m", t=PACK),
                in_=wa_raw[:].bitcast(U16).rearrange("p (m t) -> p t m", t=PACK),
            )
            for h in range(2):
                nc.vector.tensor_copy(x_plane[h][:], xs_window[:].indirect(lists[h]))

        later = ctx.enter_context(tc.tile_pool(name="later", bufs=1))
        wb_codes = later.tile([P, N], U32, name="wb_codes", align_bytes=64)
        wb_plane = later.tile([P, N], U8, name="wb_plane", align_bytes=64)
        rw_rows = later.tile([P, J], F32, name="rw_rows", align_bytes=64)
        nc.sync.dma_start(
            out=wb_codes[:].bitcast(I32), in_=wb_words[0].rearrange("p c t -> p (c t)").bitcast(I32)
        )
        for q in range(4):
            fill_scale_quadrant(nc.sync, wb_plane, wb_scales, q)
        nc.sync.dma_start(out=rw_rows[:], in_=rw[0].partition_broadcast(P))

        wa_plane = keep.tile([P, R], U8, name="wa_plane", align_bytes=64)
        nc.vector.tensor_copy(
            out=wa_plane[:].rearrange("p (t m) -> p t m", t=PACK),
            in_=was_raw[:].rearrange("p (m t) -> p t m", t=PACK),
        )
        picked = keep.tile([P, J], U32, name="picked", tag="late", align_bytes=64)
        x_codes = [picked[:, HALF * h : HALF * (h + 1)] for h in range(2)]
        for h in range(2):
            nc.vector.tensor_copy(x_codes[h], x_window[:].indirect(lists[h]))

        out_view = out.rearrange("(u p) j -> p u j", p=P)
        a_bank, mean, hid_codes, hid_plane, hid = {}, {}, {}, {}, {}

        def first_product(c):
            h, cols = c // 2, slice((c % 2) * CHUNK, (c % 2 + 1) * CHUNK)
            a_bank[c] = psum.tile([P, PACK, CHUNK], F32, name="a%d" % c, tag="a%d" % c)
            for t in range(PACK):
                nc.tensor.matmul_mx(
                    out=a_bank[c][:, t, :],
                    lhsT=wa_codes[:, 2 * P * t : 2 * P * (t + 1)].bitcast(FP4X4),
                    lhsT_scale=wa_plane[:, P * t : P * (t + 1)],
                    rhs=x_codes[h][:, cols].bitcast(FP8X4),
                    rhs_scale=x_plane[h][:, cols],
                    start=True,
                    stop=True,
                )

        def group_mean(c):
            total = keep.tile([P, CHUNK // GROUP, PACK], F32, name="total%d" % c)
            nc.vector.tensor_reduce(
                out=total[:],
                in_=a_bank[c][:].rearrange("p t (b i) -> p b t i", i=GROUP),
                axis=mybir.AxisListType.X,
                op=ALU.add,
            )
            mean[c] = keep.tile([P, CHUNK // GROUP, PACK], F32, name="mean%d" % c)
            nc.scalar.activation(out=mean[c][:], in_=total[:], func=ACT.Copy, scale=1.0 / GROUP)

        def group_mean_aside(c):
            quarter = keep.tile([P, GROUP, CHUNK], F32, name="quarter%d" % c)
            nc.scalar.activation(
                out=quarter[:].rearrange("p i (b t) -> p i b t", t=PACK),
                in_=a_bank[c][:].rearrange("p t (b i) -> p i b t", i=GROUP),
                func=ACT.Copy,
                scale=1.0 / GROUP,
            )
            pair = keep.tile([P, 2, CHUNK], F32, name="pair%d" % c)
            nc.gpsimd.tensor_tensor(out=pair[:], in0=quarter[:, 0:2, :], in1=quarter[:, 2:4, :], op=ALU.add)
            mean[c] = keep.tile([P, CHUNK // GROUP, PACK], F32, name="mean%d" % c)
            nc.gpsimd.tensor_tensor(
                out=mean[c][:].rearrange("p b t -> p (b t)"), in0=pair[:, 0, :], in1=pair[:, 1, :], op=ALU.add
            )

        def subtract(c):
            hid[c] = keep.tile([P, CHUNK * PACK], BF16, name="hid%d" % c, align_bytes=64)
            nc.vector.tensor_tensor(
                out=hid[c][:].rearrange("p (b i t) -> p b i t", i=GROUP, t=PACK),
                in0=a_bank[c][:].rearrange("p t (b i) -> p b i t", i=GROUP),
                in1=mean[c][:].unsqueeze(2).to_broadcast([P, CHUNK // GROUP, GROUP, PACK]),
                op=ALU.subtract,
            )

        def quantise(c):
            hid_codes[c] = keep.tile([P, CHUNK], U32, name="hid_codes%d" % c, align_bytes=64)
            hid_plane[c] = keep.tile([P, CHUNK], U8, name="hid_plane%d" % c, align_bytes=64)
            nc.vector.quantize_mx(out=hid_codes[c][:].bitcast(FP8X4), scales=hid_plane[c][:], in_=hid[c][:])

        p_bank = {}

        def second_product(c):
            p_bank[c] = psum.tile([P, N // P, CHUNK], F32, name="p%d" % c, tag="p%d" % c)
            for u in range(N // P):
                nc.tensor.matmul_mx(
                    out=p_bank[c][:, u, :],
                    lhsT=wb_codes[:, P * u : P * (u + 1)].bitcast(FP8X4),
                    lhsT_scale=wb_plane[:, P * u : P * (u + 1)],
                    rhs=hid_codes[c][:].bitcast(FP8X4),
                    rhs_scale=hid_plane[c][:],
                    start=True,
                    stop=True,
                )

        def last_product(c):
            halves = []
            for h, tag in enumerate(("p%d" % c, "a0")):
                halves.append(psum.tile([P, 2, CHUNK], F32, name="last%d" % h, tag=tag))
                for u in range(2 * h, 2 * h + 2):
                    nc.tensor.matmul_mx(
                        out=halves[h][:, u - 2 * h, :],
                        lhsT=wb_codes[:, P * u : P * (u + 1)].bitcast(FP8X4),
                        lhsT_scale=wb_plane[:, P * u : P * (u + 1)],
                        rhs=hid_codes[c][:].bitcast(FP8X4),
                        rhs_scale=hid_plane[c][:],
                        start=True,
                        stop=True,
                    )
            p_bank[c] = halves

        def last_weigh_and_store(c):
            cols = slice(c * CHUNK, (c + 1) * CHUNK)
            for h, queue in enumerate((nc.sync, nc.scalar)):
                result = keep.tile([P, 2, CHUNK], F32, name="last_result%d" % h)
                nc.vector.tensor_tensor(
                    out=result[:],
                    in0=p_bank[c][h][:],
                    in1=rw_rows[:, cols].unsqueeze(1).to_broadcast([P, 2, CHUNK]),
                    op=ALU.mult,
                )
                queue.dma_start(out=out_view[:, 2 * h : 2 * h + 2, cols], in_=result[:])

        def weigh_and_store(c):
            cols = slice(c * CHUNK, (c + 1) * CHUNK)
            result = keep.tile([P, N // P, CHUNK], F32, name="result%d" % c)
            nc.vector.tensor_tensor(
                out=result[:],
                in0=p_bank[c][:],
                in1=rw_rows[:, cols].unsqueeze(1).to_broadcast([P, N // P, CHUNK]),
                op=ALU.mult,
            )
            nc.sync.dma_start(out=out_view[:, :, cols], in_=result[:])

        for c in range(CHUNKS):
            first_product(c)
        group_mean(0)
        group_mean(1)
        group_mean_aside(3)
        subtract(0)
        group_mean(2)
        quantise(0)
        second_product(0)
        subtract(1)
        quantise(1)
        second_product(1)
        subtract(2)
        weigh_and_store(0)
        quantise(2)
        second_product(2)
        subtract(3)
        weigh_and_store(1)
        quantise(3)
        last_product(3)
        weigh_and_store(2)
        last_weigh_and_store(3)
